import numpy as np
import ml_dtypes


def mxq(x, axis, fmt="e4m3"):
    dtype, down = {"e4m3": (ml_dtypes.float8_e4m3fn, 7), "e5m2": (ml_dtypes.float8_e5m2, 14)}[fmt]
    v = np.moveaxis(np.asarray(x, np.float32).astype(ml_dtypes.bfloat16).astype(np.float64), axis, -1)
    blocks = v.reshape(v.shape[:-1] + (-1, 32))
    amax = np.abs(blocks).max(-1, keepdims=True)
    byte = np.maximum(np.where(amax > 0, np.frexp(amax)[1] - 1 + 127, 0) - down, 1)
    scale = np.exp2(byte - 127.0)
    codes = (blocks / scale).astype(np.float32).astype(dtype).astype(np.float64)
    return np.moveaxis((codes * scale).reshape(v.shape), -1, axis)


WIDE = False


def mx_kscale(k):
    if not WIDE:
        return np.ones(k)
    levels = np.array([30, -30])
    if k % 512:
        return np.exp2(np.random.permutation(np.resize(levels, k // 32))).repeat(32)
    a = np.empty((k // 512, 16))
    for p in range(k // 512):
        a[p, :8] = np.random.permutation(np.resize(levels, 8))
        for g in range(8):
            far = levels[np.abs(levels - a[p, g]) >= 10]
            a[p, g + 8] = far[np.random.randint(len(far))]
    return np.exp2(a.ravel()).repeat(32)


def f64(x):
    return np.asarray(x).astype(np.float64)


def striped(idx):
    return np.tile(np.asarray(idx).reshape(-1, 16).T, (8, 1)).astype(np.uint16)


def unstriped(offs):
    return offs[:16].T.reshape(-1).astype(np.int64)


E2M1 = np.array([0.0, 0.5, 1.0, 1.5, 2.0, 3.0, 4.0, 6.0, -0.0, -0.5, -1.0, -1.5, -2.0, -3.0, -4.0, -6.0])


def pack_weight(w, fmt):
    k, n = w.shape
    w = f64(np.asarray(w, np.float32).astype(ml_dtypes.bfloat16)).reshape(k // 32, 32, n)
    amax = np.abs(w).max(1)
    if fmt in ("e4m3", "e5m2"):
        byte = np.frexp(amax)[1] - 1 + 127 - (7 if fmt == "e4m3" else 14)
    else:
        mant, ex = np.frexp(amax / 6.0)
        byte = np.where(mant > 0.5, ex, ex - 1) + 127
    byte = np.clip(np.where(amax > 0, byte, 1), 1, 254)
    scaled = (w * np.exp2(127.0 - byte)[:, None, :]).reshape(k, n).astype(np.float32)
    by_word = np.ascontiguousarray(scaled.reshape(k // 512, 128, 4, n).transpose(0, 1, 3, 2))
    if fmt in ("e4m3", "e5m2"):
        words = by_word.astype(ml_dtypes.float8_e4m3fn if fmt == "e4m3" else ml_dtypes.float8_e5m2).view(np.uint8)
    else:
        c = by_word.astype(ml_dtypes.float4_e2m1fn).view(np.uint8) & 0xF
        words = (c[..., 0::2] | (c[..., 1::2] << 4)).reshape(k // 512, 128, 2 * n)
    return np.ascontiguousarray(words), np.ascontiguousarray(byte.astype(np.uint8).reshape(k // 512, 16, n))


def unpack_weight(words, scales, fmt):
    g, _, n = scales.shape
    words = np.ascontiguousarray(words).reshape(g, 128, n, -1)
    if fmt in ("e4m3", "e5m2"):
        vals = words.view(ml_dtypes.float8_e4m3fn if fmt == "e4m3" else ml_dtypes.float8_e5m2).astype(np.float64)
    else:
        nib = np.empty((g, 128, n, 4), np.uint8)
        nib[..., 0::2] = words & 0xF
        nib[..., 1::2] = words >> 4
        vals = E2M1[nib]
    vals = vals * np.repeat(np.exp2(scales.astype(np.float64) - 127.0), 8, axis=1)[..., None]
    return vals.transpose(0, 1, 3, 2).reshape(g * 512, n)


def sigmoid(v):
    return 1.0 / (1.0 + np.exp(-v))


K, T, J, R, O, N, L, E = 512, 1024, 256, 512, 128, 256, 512, 1024


def setup_inputs():
    n = np.random.standard_normal
    idx = np.random.permutation(T)[:J]
    idx2 = np.random.permutation(J)[:O]
    idx3 = np.random.permutation(J)[:O]
    idx4 = np.random.permutation(E)[:O]
    fk = mx_kscale(K)
    fr = mx_kscale(R)
    fl = mx_kscale(L)
    xtp = pack_weight(n((K, T)) / fk[:, None], "e2m1")
    wp = pack_weight(n((K, R)) * 1 / np.sqrt(K) * fk[:, None], "e5m2")
    w2p = pack_weight(n((K, R)) * 1 / np.sqrt(K) * fk[:, None] * fr, "e4m3")
    wbp = pack_weight(n((R, N)) * 1 / np.sqrt(R) / fr[:, None], "e4m3")
    sxp = pack_weight(n((L, O)) / fl[:, None], "e5m2")
    wsp = pack_weight(n((L, N)) * 1 / np.sqrt(L) * fl[:, None], "e4m3")
    return {
        "xt_words": xtp[0],
        "xt_scales": xtp[1],
        "w_words": wp[0],
        "w_scales": wp[1],
        "w2_words": w2p[0],
        "w2_scales": w2p[1],
        "sg": (np.random.uniform(0.6, 1.6, (R, 1))).astype(np.float32),
        "wb_words": wbp[0],
        "wb_scales": wbp[1],
        "sx_words": sxp[0],
        "sx_scales": sxp[1],
        "ws_words": wsp[0],
        "ws_scales": wsp[1],
        "offs": striped(idx),
        "offs2": striped(idx2),
        "offs3": striped(idx3),
        "offs4": striped(idx4),
    }


def reference(xt_words, xt_scales, w_words, w_scales, w2_words, w2_scales, sg, wb_words, wb_scales, sx_words, sx_scales, ws_words, ws_scales, offs, offs2, offs3, offs4):
    idx = unstriped(offs)
    idx2 = unstriped(offs2)
    idx3 = unstriped(offs3)
    idx4 = unstriped(offs4)
    xtu = unpack_weight(xt_words, xt_scales, "e2m1")
    wu = unpack_weight(w_words, w_scales, "e5m2")
    w2u = unpack_weight(w2_words, w2_scales, "e4m3")
    wbu = unpack_weight(wb_words, wb_scales, "e4m3")
    sxu = unpack_weight(sx_words, sx_scales, "e5m2")
    wsu = unpack_weight(ws_words, ws_scales, "e4m3")
    xtidxg = xtu[:, idx]
    a = wu.T @ xtidxg
    b = w2u.T @ xtidxg
    hid = np.maximum(b[:, idx2], b[:, idx3]) * sigmoid(a[:, idx3] * f64(sg))
    hidq = mxq(hid, 0, "e5m2")
    p = wbu.T @ hidq + wsu.T @ sxu
    y = np.zeros((N, E))
    y[:, idx4] = p
    return y

@@ -1,0 +1,194 @@
+from contextlib import ExitStack
+
+import concourse.mybir as mybir
+
+K, T, J, R, O, N, L, E = 512, 1024, 256, 512, 128, 256, 512, 1024
+FLOPS = 2 * (2 * K * R * J + R * N * O + L * N * O)
+
+F32 = mybir.dt.float32
+BF16 = mybir.dt.bfloat16
+I32 = mybir.dt.int32
+U32 = mybir.dt.uint32
+U16 = mybir.dt.uint16
+U8 = mybir.dt.uint8
+E4M3 = mybir.dt.float8_e4m3fn_x4
+E5M2 = mybir.dt.float8_e5m2_x4
+E2M1 = mybir.dt.float4_e2m1fn_x4
+ACT = mybir.ActivationFunctionType
+ALU = mybir.AluOpType
+
+P = 128
+PACK = 4
+
+
+def load_words(queue, tile, words):
+    queue.dma_start(out=tile[:, :].bitcast(I32), in_=words[0].rearrange("p c r -> p (c r)").bitcast(I32))
+
+
+def tile_list_twow_agree_skip_scattered_kernel(
+    tc, xt_words, xt_scales, w_words, w_scales, w2_words, w2_scales, sg, wb_words, wb_scales,
+    sx_words, sx_scales, ws_words, ws_scales, offs, offs2, offs3, offs4, out,
+):
+    nc = tc.nc
+    with ExitStack() as ctx:
+        sb = ctx.enter_context(tc.tile_pool(name="sb", bufs=1))
+        ps = ctx.enter_context(tc.psum_pool(name="ps", bufs=1))
+
+        def tile(name, shape, dtype, tag=""):
+            return sb.tile(shape, dtype, name=name, tag=tag, align_bytes=64)
+
+        idx = tile("idx", [P, J // 16], U16)
+        idx2 = tile("idx2", [P, O // 16], U16)
+        idx3 = tile("idx3", [P, O // 16], U16)
+        idx4 = tile("idx4", [P, O // 16], U16)
+        xt_w = tile("xt_w", [P, T], U16)
+        xt_s = tile("xt_s", [P, T], U8)
+        w_w = tile("w_w", [P, R], U32, tag="w_w")
+        w2_w = tile("w2_w", [P, R], U32, tag="w2_w")
+        rows_s = tile("rows_s", [P, 2 * R], U8)
+        late_s = tile("late_s", [P, 2 * N + O], U8)
+        wb_s, ws_s, sx_s = late_s[:, 0:N], late_s[:, N : 2 * N], late_s[:, 2 * N : 2 * N + O]
+        slope = tile("slope", [P, PACK], F32)
+        pages = [tile("page%d" % h, [P, E], F32) for h in range(2)]
+
+        for plane in (rows_s, xt_s, late_s):
+            nc.vector.memset(plane[:].bitcast(I32), 0)
+        for page in pages:
+            nc.vector.memset(page[:], 0.0)
+
+        def load_quadrant(queue, q):
+            queue.dma_start(out=xt_s[32 * q : 32 * q + 4, :].bitcast(I32), in_=xt_scales[0, 4 * q : 4 * q + 4, :].bitcast(I32))
+
+        nc.sync.dma_start(out=xt_w[:].bitcast(I32), in_=xt_words[0].bitcast(I32))
+        nc.scalar.dma_start(out=rows_s[0:16, 0:R].bitcast(I32), in_=w_scales[0].bitcast(I32))
+        nc.scalar.dma_start(out=rows_s[0:16, R : 2 * R].bitcast(I32), in_=w2_scales[0].bitcast(I32))
+        for q in range(4):
+            load_quadrant(nc.sync if q < 2 else nc.scalar, q)
+        nc.sync.dma_start(idx[:], offs)
+        load_words(nc.sync, w2_w, w2_words)
+        load_words(nc.sync, w_w, w_words)
+        nc.sync.dma_start(idx2[:], offs2)
+        nc.sync.dma_start(idx3[:], offs3)
+        nc.sync.dma_start(out=slope[:], in_=sg.rearrange("(p t) o -> p (t o)", t=PACK))
+
+        dealt_s = tile("dealt_s", [P, 2 * R], U8)
+        nc.vector.tensor_copy(
+            out=dealt_s[:].rearrange("p (w t q) -> p w q t", w=2, t=PACK),
+            in_=rows_s[:].rearrange("p (w q t) -> p w q t", w=2, t=PACK),
+        )
+        for q in range(1, 4):
+            nc.sync.dma_start(out=dealt_s[32 * q : 32 * q + 4, :].bitcast(I32), in_=dealt_s[4 * q : 4 * q + 4, :].bitcast(I32))
+        wd_s, w2d_s = dealt_s[:, 0:R], dealt_s[:, R : 2 * R]
+
+        xg_w = tile("xg_w", [P, J], U16)
+        xg_s = tile("xg_s", [P, J], U8)
+        nc.vector.tensor_copy(xg_s[:], xt_s[:].indirect(idx[:]))
+        nc.vector.tensor_copy(xg_w[:], xt_w[:].indirect(idx[:]))
+
+        def deal(name, src):
+            dst = tile(name, [P, R], U32)
+            nc.vector.tensor_copy(
+                out=dst[:].rearrange("p (t q) -> p q t", t=PACK), in_=src[:].rearrange("p (q t) -> p q t", t=PACK)
+            )
+            return dst
+
+        w2d_w = deal("w2d_w", w2_w)
+        wd_w = deal("wd_w", w_w)
+
+        late_w = tile("late_w", [P, 2 * N + O], U32, tag="w2_w")
+        wb_w, ws_w, sx_w = late_w[:, 0:N], late_w[:, N : 2 * N], late_w[:, 2 * N : 2 * N + O]
+        late_rows = tile("late_rows", [16, 2 * N + O], U8, tag="w_w")
+        for dst, src in ((ws_w, ws_words), (sx_w, sx_words), (wb_w, wb_words)):
+            load_words(nc.sync, dst, src)
+        for first, src in ((0, wb_scales), (N, ws_scales), (2 * N, sx_scales)):
+            nc.sync.dma_start(out=late_rows[:, first : first + src.shape[2]].bitcast(I32), in_=src[0].bitcast(I32))
+        for q in range(4):
+            nc.sync.dma_start(out=late_s[32 * q : 32 * q + 4, :].bitcast(I32), in_=late_rows[4 * q : 4 * q + 4, :].bitcast(I32))
+
+        nc.sync.dma_start(idx4[:], offs4)
+
+        def first_stage(bank, words, plane, fmt, t):
+            cols = slice(P * t, P * (t + 1))
+            nc.tensor.matmul_mx(
+                out=bank, lhsT=words[:, cols].bitcast(fmt), lhsT_scale=plane[:, cols],
+                rhs=xg_w[:].bitcast(E2M1), rhs_scale=xg_s[:], start=True, stop=True,
+            )
+
+        gate = tile("gate", [P, PACK, O], F32)
+        pick2 = tile("pick2", [P, PACK, O], F32)
+        pick3 = tile("pick3", [P, PACK, O], F32)
+        larger = tile("larger", [P, PACK, O], F32)
+        a_sb = [tile("a_sb%d" % t, [P, J], F32) for t in range(PACK)]
+        b_sb = [tile("b_sb%d" % t, [P, J], F32) for t in range(PACK)]
+
+        def product_a(t):
+            a_ps = ps.tile([P, J], F32, name="a_ps%d" % t)
+            first_stage(a_ps[:], wd_w, wd_s, E5M2, t)
+            nc.scalar.copy(a_sb[t][:], a_ps[:])
+
+        def product_b(t, copy):
+            b_ps = ps.tile([P, J], F32, name="b_ps%d" % t)
+            first_stage(b_ps[:], w2d_w, w2d_s, E4M3, t)
+            copy(b_sb[t][:], b_ps[:])
+
+        def look(t):
+            nc.scalar.activation(out=gate[:, t, :], in_=a_sb[t][:].indirect(idx3[:]), func=ACT.Sigmoid, scale=slope[:, t : t + 1])
+
+        def picks(t):
+            nc.vector.tensor_copy(pick2[:, t, :], b_sb[t][:].indirect(idx2[:]))
+            if t == PACK - 1:
+                nc.scalar.activation(out=pick3[:, t, :], in_=b_sb[t][:].indirect(idx3[:]), func=ACT.Copy)
+            else:
+                nc.vector.tensor_copy(pick3[:, t, :], b_sb[t][:].indirect(idx3[:]))
+            if t % 2 == 1:
+                pair = slice(t - 1, t + 1)
+                nc.vector.tensor_tensor(larger[:, pair, :], pick2[:, pair, :], pick3[:, pair, :], ALU.max)
+
+        product_b(0, nc.vector.tensor_copy)
+        product_a(0)
+        product_b(1, nc.vector.tensor_copy)
+        product_b(2, nc.scalar.copy)
+        picks(0)
+        look(0)
+        product_a(1)
+        product_b(3, nc.scalar.copy)
+        picks(1)
+        look(1)
+        product_a(2)
+        picks(2)
+        picks(3)
+        product_a(3)
+        look(2)
+        look(3)
+
+        hid = tile("hid", [P, O * PACK], BF16)
+        nc.vector.tensor_tensor(
+            hid[:].rearrange("p (c i t) -> p c t i", i=4, t=PACK),
+            larger[:].rearrange("p t (c i) -> p c t i", i=4),
+            gate[:].rearrange("p t (c i) -> p c t i", i=4),
+            ALU.mult,
+        )
+        hq_w = tile("hq_w", [P, O], U32)
+        hq_s = tile("hq_s", [P, O], U8)
+        nc.vector.quantize_mx(out=hq_w[:].bitcast(E5M2), scales=hq_s[:], in_=hid[:])
+
+        for h in range(2):
+            cols = slice(P * h, P * (h + 1))
+            p_ps = ps.tile([P, O], F32, name="p_ps%d" % h, tag="a_ps%d" % h)
+            nc.tensor.matmul_mx(
+                out=p_ps[:], lhsT=ws_w[:, cols].bitcast(E4M3), lhsT_scale=ws_s[:, cols],
+                rhs=sx_w.bitcast(E5M2), rhs_scale=sx_s, start=True, stop=False,
+            )
+            nc.tensor.matmul_mx(
+                out=p_ps[:], lhsT=wb_w[:, cols].bitcast(E4M3), lhsT_scale=wb_s[:, cols],
+                rhs=hq_w[:].bitcast(E5M2), rhs_scale=hq_s[:], start=False, stop=True,
+            )
+            p_sb = tile("p_sb%d" % h, [P, O], F32)
+            if h == 0:
+                nc.vector.tensor_copy(p_sb[:], p_ps[:])
+                nc.vector.tensor_copy(pages[h][:].indirect(idx4[:]), p_sb[:])
+                nc.sync.dma_start(out=out[cols, :], in_=pages[h][:])
+            else:
+                nc.scalar.copy(p_sb[:], p_ps[:])
+                nc.scalar.activation(out=pages[h][:].indirect(idx4[:]), in_=p_sb[:], func=ACT.Copy)
+                nc.scalar.dma_start(out=out[cols, :], in_=pages[h][:])

@@ -53,6 +53,8 @@ def tile_list_twow_agree_skip_scattered_kernel(
 
         for plane in (rows_s, xt_s, late_s):
             nc.vector.memset(plane[:].bitcast(I32), 0)
+        warm = tile("warm", [P, 8], F32)
+        nc.vector.memset(warm[:, 0:1], 0.0)
         for page in pages:
             nc.vector.memset(page[:], 0.0)
 
@@ -70,6 +72,8 @@ def tile_list_twow_agree_skip_scattered_kernel(
         nc.sync.dma_start(idx2[:], offs2)
         nc.sync.dma_start(idx3[:], offs3)
         nc.sync.dma_start(out=slope[:], in_=sg.rearrange("(p t) o -> p (t o)", t=PACK))
+
+        nc.scalar.activation(out=warm[:, 1:2], in_=warm[:, 0:1], func=ACT.Sigmoid)
 
         dealt_s = tile("dealt_s", [P, 2 * R], U8)
         nc.vector.tensor_copy(

@@ -43,73 +43,70 @@ def tile_list_twow_agree_skip_scattered_kernel(
         idx4 = tile("idx4", [P, O // 16], U16)
         xt_w = tile("xt_w", [P, T], U16)
         xt_s = tile("xt_s", [P, T], U8)
-        w_w = tile("w_w", [P, R], U32, tag="w_w")
-        w2_w = tile("w2_w", [P, R], U32, tag="w2_w")
+        w_w = tile("w_w", [P, R], U32)
+        w2_w = tile("w2_w", [P, R], U32)
         rows_s = tile("rows_s", [P, 2 * R], U8)
         late_s = tile("late_s", [P, 2 * N + O], U8)
         wb_s, ws_s, sx_s = late_s[:, 0:N], late_s[:, N : 2 * N], late_s[:, 2 * N : 2 * N + O]
         slope = tile("slope", [P, PACK], F32)
         pages = [tile("page%d" % h, [P, E], F32) for h in range(2)]
 
-        for plane in (rows_s, xt_s, late_s):
-            nc.vector.memset(plane[:].bitcast(I32), 0)
+        late_w = tile("late_w", [P, 2 * N + O], U32)
+        wb_w, ws_w, sx_w = late_w[:, 0:N], late_w[:, N : 2 * N], late_w[:, 2 * N : 2 * N + O]
         warm = tile("warm", [P, 8], F32)
+
+        nc.vector.memset(rows_s[:].bitcast(I32), 0)
+        nc.vector.memset(xt_s[:].bitcast(I32), 0)
         nc.vector.memset(warm[:, 0:1], 0.0)
+        nc.vector.memset(late_s[:].bitcast(I32), 0)
         for page in pages:
             nc.vector.memset(page[:], 0.0)
 
-        def load_quadrant(queue, q):
-            queue.dma_start(out=xt_s[32 * q : 32 * q + 4, :].bitcast(I32), in_=xt_scales[0, 4 * q : 4 * q + 4, :].bitcast(I32))
+        def spread(queue, plane):
+            for q in range(1, 4):
+                queue.dma_start(out=plane[32 * q : 32 * q + 4, :].bitcast(I32), in_=plane[4 * q : 4 * q + 4, :].bitcast(I32))
 
-        nc.sync.dma_start(out=xt_w[:].bitcast(I32), in_=xt_words[0].bitcast(I32))
-        nc.scalar.dma_start(out=rows_s[0:16, 0:R].bitcast(I32), in_=w_scales[0].bitcast(I32))
-        nc.scalar.dma_start(out=rows_s[0:16, R : 2 * R].bitcast(I32), in_=w2_scales[0].bitcast(I32))
-        for q in range(4):
-            load_quadrant(nc.sync if q < 2 else nc.scalar, q)
+        def load_xt_quadrant(q):
+            nc.sync.dma_start(out=xt_s[32 * q : 32 * q + 4, :].bitcast(I32), in_=xt_scales[0, 4 * q : 4 * q + 4, :].bitcast(I32))
+
         nc.sync.dma_start(idx[:], offs)
+        nc.scalar.dma_start(out=rows_s[0:16, R : 2 * R].bitcast(I32), in_=w2_scales[0].bitcast(I32))
+        nc.scalar.dma_start(out=rows_s[0:16, 0:R].bitcast(I32), in_=w_scales[0].bitcast(I32))
+        nc.scalar.activation(out=warm[:, 1:2], in_=warm[:, 0:1], func=ACT.Sigmoid)
+        spread(nc.scalar, rows_s)
+        load_xt_quadrant(0)
+        nc.sync.dma_start(out=xt_w[:].bitcast(I32), in_=xt_words[0].bitcast(I32))
         load_words(nc.sync, w2_w, w2_words)
         load_words(nc.sync, w_w, w_words)
+        for q in range(1, 4):
+            load_xt_quadrant(q)
         nc.sync.dma_start(idx2[:], offs2)
         nc.sync.dma_start(idx3[:], offs3)
         nc.sync.dma_start(out=slope[:], in_=sg.rearrange("(p t) o -> p (t o)", t=PACK))
-
-        nc.scalar.activation(out=warm[:, 1:2], in_=warm[:, 0:1], func=ACT.Sigmoid)
-
-        dealt_s = tile("dealt_s", [P, 2 * R], U8)
-        nc.vector.tensor_copy(
-            out=dealt_s[:].rearrange("p (w t q) -> p w q t", w=2, t=PACK),
-            in_=rows_s[:].rearrange("p (w q t) -> p w q t", w=2, t=PACK),
-        )
-        for q in range(1, 4):
-            nc.sync.dma_start(out=dealt_s[32 * q : 32 * q + 4, :].bitcast(I32), in_=dealt_s[4 * q : 4 * q + 4, :].bitcast(I32))
-        wd_s, w2d_s = dealt_s[:, 0:R], dealt_s[:, R : 2 * R]
+        for dst, src in ((wb_s, wb_scales), (ws_s, ws_scales), (sx_s, sx_scales)):
+            nc.sync.dma_start(out=dst[0:16, :].bitcast(I32), in_=src[0].bitcast(I32))
+        spread(nc.sync, late_s)
+        for dst, src in ((ws_w, ws_words), (sx_w, sx_words), (wb_w, wb_words)):
+            load_words(nc.sync, dst, src)
+        nc.sync.dma_start(idx4[:], offs4)
 
         xg_w = tile("xg_w", [P, J], U16)
         xg_s = tile("xg_s", [P, J], U8)
-        nc.vector.tensor_copy(xg_s[:], xt_s[:].indirect(idx[:]))
-        nc.vector.tensor_copy(xg_w[:], xt_w[:].indirect(idx[:]))
 
-        def deal(name, src):
-            dst = tile(name, [P, R], U32)
+        def deal(name, src, dtype, run):
+            dst = tile(name, [P, R], dtype)
             nc.vector.tensor_copy(
-                out=dst[:].rearrange("p (t q) -> p q t", t=PACK), in_=src[:].rearrange("p (q t) -> p q t", t=PACK)
+                out=dst[:].rearrange("p (t c i) -> p c t i", t=PACK, i=run),
+                in_=src.rearrange("p (c i t) -> p c t i", t=PACK, i=run),
             )
             return dst
 
-        w2d_w = deal("w2d_w", w2_w)
-        wd_w = deal("wd_w", w_w)
-
-        late_w = tile("late_w", [P, 2 * N + O], U32, tag="w2_w")
-        wb_w, ws_w, sx_w = late_w[:, 0:N], late_w[:, N : 2 * N], late_w[:, 2 * N : 2 * N + O]
-        late_rows = tile("late_rows", [16, 2 * N + O], U8, tag="w_w")
-        for dst, src in ((ws_w, ws_words), (sx_w, sx_words), (wb_w, wb_words)):
-            load_words(nc.sync, dst, src)
-        for first, src in ((0, wb_scales), (N, ws_scales), (2 * N, sx_scales)):
-            nc.sync.dma_start(out=late_rows[:, first : first + src.shape[2]].bitcast(I32), in_=src[0].bitcast(I32))
-        for q in range(4):
-            nc.sync.dma_start(out=late_s[32 * q : 32 * q + 4, :].bitcast(I32), in_=late_rows[4 * q : 4 * q + 4, :].bitcast(I32))
-
-        nc.sync.dma_start(idx4[:], offs4)
+        nc.vector.tensor_copy(xg_w[:], xt_w[:].indirect(idx[:]))
+        w2d_w = deal("w2d_w", w2_w[:], U32, 4)
+        wd_w = deal("wd_w", w_w[:], U32, 4)
+        nc.vector.tensor_copy(xg_s[:], xt_s[:].indirect(idx[:]))
+        w2d_s = deal("w2d_s", rows_s[:, R : 2 * R], U8, 16)
+        wd_s = deal("wd_s", rows_s[:, 0:R], U8, 16)
 
         def first_stage(bank, words, plane, fmt, t):
             cols = slice(P * t, P * (t + 1))
@@ -125,6 +122,8 @@ def tile_list_twow_agree_skip_scattered_kernel(
         a_sb = [tile("a_sb%d" % t, [P, J], F32) for t in range(PACK)]
         b_sb = [tile("b_sb%d" % t, [P, J], F32) for t in range(PACK)]
 
+        half = O // 2
+
         def product_a(t):
             a_ps = ps.tile([P, J], F32, name="a_ps%d" % t)
             first_stage(a_ps[:], wd_w, wd_s, E5M2, t)
@@ -135,50 +134,48 @@ def tile_list_twow_agree_skip_scattered_kernel(
             first_stage(b_ps[:], w2d_w, w2d_s, E4M3, t)
             copy(b_sb[t][:], b_ps[:])
 
-        def look(t):
-            nc.scalar.activation(out=gate[:, t, :], in_=a_sb[t][:].indirect(idx3[:]), func=ACT.Sigmoid, scale=slope[:, t : t + 1])
+        def look(t, first, count):
+            nc.scalar.activation(
+                out=gate[:, t, first : first + count], in_=a_sb[t][:].indirect(idx3[:, first // 16 : (first + count) // 16]),
+                func=ACT.Sigmoid, scale=slope[:, t : t + 1],
+            )
 
-        def picks(t):
-            nc.vector.tensor_copy(pick2[:, t, :], b_sb[t][:].indirect(idx2[:]))
-            if t == PACK - 1:
-                nc.scalar.activation(out=pick3[:, t, :], in_=b_sb[t][:].indirect(idx3[:]), func=ACT.Copy)
-            else:
-                nc.vector.tensor_copy(pick3[:, t, :], b_sb[t][:].indirect(idx3[:]))
-            if t % 2 == 1:
-                pair = slice(t - 1, t + 1)
-                nc.vector.tensor_tensor(larger[:, pair, :], pick2[:, pair, :], pick3[:, pair, :], ALU.max)
-
-        product_b(0, nc.vector.tensor_copy)
+        product_b(0, nc.scalar.copy)
+        for t in range(1, PACK):
+            product_b(t, nc.vector.tensor_copy)
+        for dst, lst in ((pick2, idx2), (pick3, idx3)):
+            nc.scalar.activation(out=dst[:, 0, :], in_=b_sb[0][:].indirect(lst[:]), func=ACT.Copy)
+        for t in range(1, PACK):
+            for dst, lst in ((pick2, idx2), (pick3, idx3)):
+                nc.vector.tensor_copy(dst[:, t, :], b_sb[t][:].indirect(lst[:]))
         product_a(0)
-        product_b(1, nc.vector.tensor_copy)
-        product_b(2, nc.scalar.copy)
-        picks(0)
-        look(0)
-        product_a(1)
-        product_b(3, nc.scalar.copy)
-        picks(1)
-        look(1)
-        product_a(2)
-        picks(2)
-        picks(3)
-        product_a(3)
-        look(2)
-        look(3)
+        for t in range(1, PACK):
+            product_a(t)
+            look(t - 1, 0, O)
+        for u in range(2):
+            look(PACK - 1, u * half, half)
+        nc.vector.tensor_tensor(larger[:], pick2[:], pick3[:], ALU.max)
 
         hid = tile("hid", [P, O * PACK], BF16)
-        nc.vector.tensor_tensor(
-            hid[:].rearrange("p (c i t) -> p c t i", i=4, t=PACK),
-            larger[:].rearrange("p t (c i) -> p c t i", i=4),
-            gate[:].rearrange("p t (c i) -> p c t i", i=4),
-            ALU.mult,
-        )
         hq_w = tile("hq_w", [P, O], U32)
         hq_s = tile("hq_s", [P, O], U8)
-        nc.vector.quantize_mx(out=hq_w[:].bitcast(E5M2), scales=hq_s[:], in_=hid[:])
+        for u in range(2):
+            places = slice(u * half, (u + 1) * half)
+            nc.vector.tensor_tensor(
+                hid[:, PACK * places.start : PACK * places.stop].rearrange("p (c i t) -> p c t i", i=4, t=PACK),
+                larger[:, :, places].rearrange("p t (c i) -> p c t i", i=4),
+                gate[:, :, places].rearrange("p t (c i) -> p c t i", i=4),
+                ALU.mult,
+            )
+        for u in range(2):
+            places = slice(u * half, (u + 1) * half)
+            nc.vector.quantize_mx(
+                out=hq_w[:, places].bitcast(E5M2), scales=hq_s[:, places], in_=hid[:, PACK * places.start : PACK * places.stop]
+            )
 
         for h in range(2):
             cols = slice(P * h, P * (h + 1))
-            p_ps = ps.tile([P, O], F32, name="p_ps%d" % h, tag="a_ps%d" % h)
+            p_ps = ps.tile([P, O], F32, name="p_ps%d" % h, tag="b_ps%d" % h)
             nc.tensor.matmul_mx(
                 out=p_ps[:], lhsT=ws_w[:, cols].bitcast(E4M3), lhsT_scale=ws_s[:, cols],
                 rhs=sx_w.bitcast(E5M2), rhs_scale=sx_s, start=True, stop=False,

from contextlib import ExitStack

import concourse.mybir as mybir

K, T, J, R, O, N, L, E = 512, 1024, 256, 512, 128, 256, 512, 1024
FLOPS = 2 * (2 * K * R * J + R * N * O + L * N * O)

F32 = mybir.dt.float32
BF16 = mybir.dt.bfloat16
I32 = mybir.dt.int32
U32 = mybir.dt.uint32
U16 = mybir.dt.uint16
U8 = mybir.dt.uint8
E4M3 = mybir.dt.float8_e4m3fn_x4
E5M2 = mybir.dt.float8_e5m2_x4
E2M1 = mybir.dt.float4_e2m1fn_x4
ACT = mybir.ActivationFunctionType
ALU = mybir.AluOpType

P = 128
PACK = 4


def load_words(queue, tile, words):
    queue.dma_start(out=tile[:, :].bitcast(I32), in_=words[0].rearrange("p c r -> p (c r)").bitcast(I32))


def tile_list_twow_agree_skip_scattered_kernel(
    tc, xt_words, xt_scales, w_words, w_scales, w2_words, w2_scales, sg, wb_words, wb_scales,
    sx_words, sx_scales, ws_words, ws_scales, offs, offs2, offs3, offs4, out,
):
    nc = tc.nc
    with ExitStack() as ctx:
        sb = ctx.enter_context(tc.tile_pool(name="sb", bufs=1))
        ps = ctx.enter_context(tc.psum_pool(name="ps", bufs=1))

        def tile(name, shape, dtype, tag=""):
            return sb.tile(shape, dtype, name=name, tag=tag, align_bytes=64)

        idx = tile("idx", [P, J // 16], U16)
        idx2 = tile("idx2", [P, O // 16], U16)
        idx3 = tile("idx3", [P, O // 16], U16)
        idx4 = tile("idx4", [P, O // 16], U16)
        xt_w = tile("xt_w", [P, T], U16)
        xt_s = tile("xt_s", [P, T], U8)
        w_w = tile("w_w", [P, R], U32)
        w2_w = tile("w2_w", [P, R], U32)
        rows_s = tile("rows_s", [P, 2 * R], U8)
        late_s = tile("late_s", [P, 2 * N + O], U8)
        wb_s, ws_s, sx_s = late_s[:, 0:N], late_s[:, N : 2 * N], late_s[:, 2 * N : 2 * N + O]
        slope = tile("slope", [P, PACK], F32)
        pages = [tile("page%d" % h, [P, E], F32) for h in range(2)]

        late_w = tile("late_w", [P, 2 * N + O], U32)
        wb_w, ws_w, sx_w = late_w[:, 0:N], late_w[:, N : 2 * N], late_w[:, 2 * N : 2 * N + O]
        warm = tile("warm", [P, 8], F32)

        nc.vector.memset(rows_s[:].bitcast(I32), 0)
        nc.vector.memset(xt_s[:].bitcast(I32), 0)
        nc.vector.memset(warm[:, 0:1], 0.0)
        nc.vector.memset(late_s[:].bitcast(I32), 0)
        for page in pages:
            nc.vector.memset(page[:], 0.0)

        def spread(queue, plane):
            for q in range(1, 4):
                queue.dma_start(out=plane[32 * q : 32 * q + 4, :].bitcast(I32), in_=plane[4 * q : 4 * q + 4, :].bitcast(I32))

        def load_xt_quadrant(q):
            nc.sync.dma_start(out=xt_s[32 * q : 32 * q + 4, :].bitcast(I32), in_=xt_scales[0, 4 * q : 4 * q + 4, :].bitcast(I32))

        nc.sync.dma_start(idx[:], offs)
        nc.scalar.dma_start(out=rows_s[0:16, R : 2 * R].bitcast(I32), in_=w2_scales[0].bitcast(I32))
        nc.scalar.dma_start(out=rows_s[0:16, 0:R].bitcast(I32), in_=w_scales[0].bitcast(I32))
        nc.scalar.activation(out=warm[:, 1:2], in_=warm[:, 0:1], func=ACT.Sigmoid)
        spread(nc.scalar, rows_s)
        load_xt_quadrant(0)
        nc.sync.dma_start(out=xt_w[:].bitcast(I32), in_=xt_words[0].bitcast(I32))
        load_words(nc.sync, w2_w, w2_words)
        load_words(nc.sync, w_w, w_words)
        for q in range(1, 4):
            load_xt_quadrant(q)
        nc.sync.dma_start(idx2[:], offs2)
        nc.sync.dma_start(idx3[:], offs3)
        nc.sync.dma_start(out=slope[:], in_=sg.rearrange("(p t) o -> p (t o)", t=PACK))
        for dst, src in ((wb_s, wb_scales), (ws_s, ws_scales), (sx_s, sx_scales)):
            nc.sync.dma_start(out=dst[0:16, :].bitcast(I32), in_=src[0].bitcast(I32))
        spread(nc.sync, late_s)
        for dst, src in ((ws_w, ws_words), (sx_w, sx_words), (wb_w, wb_words)):
            load_words(nc.sync, dst, src)
        nc.sync.dma_start(idx4[:], offs4)

        xg_w = tile("xg_w", [P, J], U16)
        xg_s = tile("xg_s", [P, J], U8)

        def deal(name, src, dtype, run):
            dst = tile(name, [P, R], dtype)
            nc.vector.tensor_copy(
                out=dst[:].rearrange("p (t c i) -> p c t i", t=PACK, i=run),
                in_=src.rearrange("p (c i t) -> p c t i", t=PACK, i=run),
            )
            return dst

        nc.vector.tensor_copy(xg_w[:], xt_w[:].indirect(idx[:]))
        w2d_w = deal("w2d_w", w2_w[:], U32, 4)
        wd_w = deal("wd_w", w_w[:], U32, 4)
        nc.vector.tensor_copy(xg_s[:], xt_s[:].indirect(idx[:]))
        w2d_s = deal("w2d_s", rows_s[:, R : 2 * R], U8, 16)
        wd_s = deal("wd_s", rows_s[:, 0:R], U8, 16)

        def first_stage(bank, words, plane, fmt, t):
            cols = slice(P * t, P * (t + 1))
            nc.tensor.matmul_mx(
                out=bank, lhsT=words[:, cols].bitcast(fmt), lhsT_scale=plane[:, cols],
                rhs=xg_w[:].bitcast(E2M1), rhs_scale=xg_s[:], start=True, stop=True,
            )

        gate = tile("gate", [P, PACK, O], F32)
        pick2 = tile("pick2", [P, PACK, O], F32)
        pick3 = tile("pick3", [P, PACK, O], F32)
        larger = tile("larger", [P, PACK, O], F32)
        a_sb = [tile("a_sb%d" % t, [P, J], F32) for t in range(PACK)]
        b_sb = [tile("b_sb%d" % t, [P, J], F32) for t in range(PACK)]

        half = O // 2

        def product_a(t):
            a_ps = ps.tile([P, J], F32, name="a_ps%d" % t)
            first_stage(a_ps[:], wd_w, wd_s, E5M2, t)
            nc.scalar.copy(a_sb[t][:], a_ps[:])

        def product_b(t, copy):
            b_ps = ps.tile([P, J], F32, name="b_ps%d" % t)
            first_stage(b_ps[:], w2d_w, w2d_s, E4M3, t)
            copy(b_sb[t][:], b_ps[:])

        def look(t, first, count):
            nc.scalar.activation(
                out=gate[:, t, first : first + count], in_=a_sb[t][:].indirect(idx3[:, first // 16 : (first + count) // 16]),
                func=ACT.Sigmoid, scale=slope[:, t : t + 1],
            )

        product_b(0, nc.scalar.copy)
        for t in range(1, PACK):
            product_b(t, nc.vector.tensor_copy)
        for dst, lst in ((pick2, idx2), (pick3, idx3)):
            nc.scalar.activation(out=dst[:, 0, :], in_=b_sb[0][:].indirect(lst[:]), func=ACT.Copy)
        for t in range(1, PACK):
            for dst, lst in ((pick2, idx2), (pick3, idx3)):
                nc.vector.tensor_copy(dst[:, t, :], b_sb[t][:].indirect(lst[:]))
        product_a(0)
        for t in range(1, PACK):
            product_a(t)
            look(t - 1, 0, O)
        for u in range(2):
            look(PACK - 1, u * half, half)
        nc.vector.tensor_tensor(larger[:], pick2[:], pick3[:], ALU.max)

        hid = tile("hid", [P, O * PACK], BF16)
        hq_w = tile("hq_w", [P, O], U32)
        hq_s = tile("hq_s", [P, O], U8)
        for u in range(2):
            places = slice(u * half, (u + 1) * half)
            nc.vector.tensor_tensor(
                hid[:, PACK * places.start : PACK * places.stop].rearrange("p (c i t) -> p c t i", i=4, t=PACK),
                larger[:, :, places].rearrange("p t (c i) -> p c t i", i=4),
                gate[:, :, places].rearrange("p t (c i) -> p c t i", i=4),
                ALU.mult,
            )
        for u in range(2):
            places = slice(u * half, (u + 1) * half)
            nc.vector.quantize_mx(
                out=hq_w[:, places].bitcast(E5M2), scales=hq_s[:, places], in_=hid[:, PACK * places.start : PACK * places.stop]
            )

        for h in range(2):
            cols = slice(P * h, P * (h + 1))
            p_ps = ps.tile([P, O], F32, name="p_ps%d" % h, tag="b_ps%d" % h)
            nc.tensor.matmul_mx(
                out=p_ps[:], lhsT=ws_w[:, cols].bitcast(E4M3), lhsT_scale=ws_s[:, cols],
                rhs=sx_w.bitcast(E5M2), rhs_scale=sx_s, start=True, stop=False,
            )
            nc.tensor.matmul_mx(
                out=p_ps[:], lhsT=wb_w[:, cols].bitcast(E4M3), lhsT_scale=wb_s[:, cols],
                rhs=hq_w[:].bitcast(E5M2), rhs_scale=hq_s[:], start=False, stop=True,
            )
            p_sb = tile("p_sb%d" % h, [P, O], F32)
            if h == 0:
                nc.vector.tensor_copy(p_sb[:], p_ps[:])
                nc.vector.tensor_copy(pages[h][:].indirect(idx4[:]), p_sb[:])
                nc.sync.dma_start(out=out[cols, :], in_=pages[h][:])
            else:
                nc.scalar.copy(p_sb[:], p_ps[:])
                nc.scalar.activation(out=pages[h][:].indirect(idx4[:]), in_=p_sb[:], func=ACT.Copy)
                nc.scalar.dma_start(out=out[cols, :], in_=pages[h][:])
